import numpy as np
import ml_dtypes

BF16 = ml_dtypes.bfloat16


def bf(x):
    return np.asarray(x, np.float32).astype(BF16)


def f32(x):
    return np.asarray(x, np.float32)


def f64(x):
    return np.asarray(x).astype(np.float64)


def striped(idx):
    return np.tile(idx.reshape(-1, 16).T, (8, 1))


S, K, M, N, E, Q = 256, 512, 128, 256, 2, 128


def setup_inputs():
    return {"base": bf(np.random.standard_normal((M, S))), "x": bf(np.random.standard_normal((K, N))), "w": bf(np.random.standard_normal((E, K, M)) / np.sqrt(K)), "offs": striped(np.random.permutation(S))}


def reference(base, x, w, offs):
    idx = offs[:16].T.reshape(-1)
    z = f64(base).copy()
    for e in range(E):
        z[:, idx[e * Q : (e + 1) * Q]] += f64(w)[e].T @ f64(x)[:, e * Q : (e + 1) * Q]
    return z

@@ -1,0 +1,52 @@
+import concourse.mybir as mybir
+from concourse.masks import make_identity
+
+BF16, F32, U16 = mybir.dt.bfloat16, mybir.dt.float32, mybir.dt.uint16
+
+P = 128
+TOKENS = 256
+K_BLOCKS = 4
+EXPERTS = 2
+PIECE = TOKENS // EXPERTS
+PIECE_COLS = PIECE // 16
+
+FLOPS = 2 * K_BLOCKS * P * P * TOKENS
+
+
+def tile_scatter_matmul_kernel(tc, base, x, w, offs, out):
+    nc = tc.nc
+    with (
+        tc.tile_pool(name="held", bufs=1) as held,
+        tc.psum_pool(name="psum", bufs=1) as psum,
+    ):
+        offsets = held.tile([P, TOKENS // 16], U16, name="offsets")
+        nc.sync.dma_start(offsets[:], offs)
+
+        base_sb = held.tile([P, TOKENS], BF16, name="base_sb")
+        nc.scalar.dma_start(base_sb[:], base)
+
+        x_sb = held.tile([P, K_BLOCKS, TOKENS], BF16, name="x_sb")
+        nc.sync.dma_start(x_sb[:], x.rearrange("(kb p) n -> p kb n", p=P))
+        w_sb = held.tile([P, EXPERTS * K_BLOCKS, P], BF16, name="w_sb")
+        nc.scalar.dma_start(w_sb[:], w.rearrange("e (kb p) m -> p (e kb) m", p=P))
+
+        ident = held.tile([P, P], BF16, name="ident")
+        make_identity(nc, ident[:])
+
+        window = psum.tile([P, TOKENS], F32, name="window")
+        nc.tensor.matmul(window[:], ident[:], base_sb[:], start=True, stop=False)
+
+        for e in range(EXPERTS):
+            piece = offsets[:, e * PIECE_COLS : (e + 1) * PIECE_COLS]
+            for kb in range(K_BLOCKS):
+                nc.tensor.matmul(
+                    window[:].indirect(piece),
+                    w_sb[:, e * K_BLOCKS + kb, :],
+                    x_sb[:, kb, e * PIECE : (e + 1) * PIECE],
+                    start=False,
+                    stop=(e == EXPERTS - 1 and kb == K_BLOCKS - 1),
+                )
+
+        z_sb = held.tile([P, TOKENS], F32, name="z_sb")
+        nc.vector.tensor_copy(z_sb[:], window[:])
+        nc.sync.dma_start(out, z_sb[:])

@@ -7,8 +7,13 @@ P = 128
 TOKENS = 256
 K_BLOCKS = 4
 EXPERTS = 2
+HALVES = 2
+HALF_BLOCKS = K_BLOCKS // HALVES
 PIECE = TOKENS // EXPERTS
 PIECE_COLS = PIECE // 16
+
+WARM_COLS = 128
+WARM_MATMULS = 10
 
 FLOPS = 2 * K_BLOCKS * P * P * TOKENS
 
@@ -25,10 +30,21 @@ def tile_scatter_matmul_kernel(tc, base, x, w, offs, out):
         base_sb = held.tile([P, TOKENS], BF16, name="base_sb")
         nc.scalar.dma_start(base_sb[:], base)
 
-        x_sb = held.tile([P, K_BLOCKS, TOKENS], BF16, name="x_sb")
-        nc.sync.dma_start(x_sb[:], x.rearrange("(kb p) n -> p kb n", p=P))
-        w_sb = held.tile([P, EXPERTS * K_BLOCKS, P], BF16, name="w_sb")
-        nc.scalar.dma_start(w_sb[:], w.rearrange("e (kb p) m -> p (e kb) m", p=P))
+        x_view = x.rearrange("(p kb) n -> p kb n", kb=K_BLOCKS)
+        w_view = w.rearrange("e (p kb) m -> p e kb m", kb=K_BLOCKS)
+        x_sb, w_sb = [], []
+        for h in range(HALVES):
+            blocks = slice(h * HALF_BLOCKS, (h + 1) * HALF_BLOCKS)
+            x_sb.append(held.tile([P, HALF_BLOCKS, TOKENS], BF16, name="x_sb%d" % h))
+            nc.sync.dma_start(x_sb[h][:], x_view[:, blocks, :])
+            w_sb.append(held.tile([P, EXPERTS, HALF_BLOCKS, P], BF16, name="w_sb%d" % h))
+            nc.scalar.dma_start(w_sb[h][:], w_view[:, :, blocks, :])
+
+        zeros = held.tile([P, WARM_COLS], BF16, name="zeros")
+        nc.gpsimd.memset(zeros[:], 0.0)
+        warm = psum.tile([P, WARM_COLS], F32, name="warm")
+        for i in range(WARM_MATMULS):
+            nc.tensor.matmul(warm[:], zeros[:, 0:P], zeros[:], start=True, stop=True)
 
         ident = held.tile([P, P], BF16, name="ident")
         make_identity(nc, ident[:])
@@ -36,15 +52,15 @@ def tile_scatter_matmul_kernel(tc, base, x, w, offs, out):
         window = psum.tile([P, TOKENS], F32, name="window")
         nc.tensor.matmul(window[:], ident[:], base_sb[:], start=True, stop=False)
 
-        for e in range(EXPERTS):
-            piece = offsets[:, e * PIECE_COLS : (e + 1) * PIECE_COLS]
-            for kb in range(K_BLOCKS):
+        for kb in range(K_BLOCKS):
+            h, b = divmod(kb, HALF_BLOCKS)
+            for e in range(EXPERTS):
                 nc.tensor.matmul(
-                    window[:].indirect(piece),
-                    w_sb[:, e * K_BLOCKS + kb, :],
-                    x_sb[:, kb, e * PIECE : (e + 1) * PIECE],
+                    window[:].indirect(offsets[:, e * PIECE_COLS : (e + 1) * PIECE_COLS]),
+                    w_sb[h][:, e, b, :],
+                    x_sb[h][:, b, e * PIECE : (e + 1) * PIECE],
                     start=False,
-                    stop=(e == EXPERTS - 1 and kb == K_BLOCKS - 1),
+                    stop=(kb == K_BLOCKS - 1 and e == EXPERTS - 1),
                 )
 
         z_sb = held.tile([P, TOKENS], F32, name="z_sb")

@@ -24,21 +24,21 @@ def tile_scatter_matmul_kernel(tc, base, x, w, offs, out):
         tc.tile_pool(name="held", bufs=1) as held,
         tc.psum_pool(name="psum", bufs=1) as psum,
     ):
+        base_sb = held.tile([P, TOKENS], BF16, name="base_sb")
+        nc.sync.dma_start(base_sb[:], base)
+
         offsets = held.tile([P, TOKENS // 16], U16, name="offsets")
         nc.sync.dma_start(offsets[:], offs)
-
-        base_sb = held.tile([P, TOKENS], BF16, name="base_sb")
-        nc.scalar.dma_start(base_sb[:], base)
 
         x_view = x.rearrange("(p kb) n -> p kb n", kb=K_BLOCKS)
         w_view = w.rearrange("e (p kb) m -> p e kb m", kb=K_BLOCKS)
         x_sb, w_sb = [], []
-        for h in range(HALVES):
-            blocks = slice(h * HALF_BLOCKS, (h + 1) * HALF_BLOCKS)
-            x_sb.append(held.tile([P, HALF_BLOCKS, TOKENS], BF16, name="x_sb%d" % h))
-            nc.sync.dma_start(x_sb[h][:], x_view[:, blocks, :])
-            w_sb.append(held.tile([P, EXPERTS, HALF_BLOCKS, P], BF16, name="w_sb%d" % h))
-            nc.scalar.dma_start(w_sb[h][:], w_view[:, :, blocks, :])
+        for i in range(HALVES):
+            blocks = slice(i * HALF_BLOCKS, (i + 1) * HALF_BLOCKS)
+            x_sb.append(held.tile([P, HALF_BLOCKS, TOKENS], BF16, name="x_sb%d" % i))
+            nc.sync.dma_start(x_sb[i][:], x_view[:, blocks, :])
+            w_sb.append(held.tile([P, K_BLOCKS, P], BF16, name="w_sb%d" % i))
+            nc.sync.dma_start(w_sb[i][:], w_view[:, i, :, :])
 
         zeros = held.tile([P, WARM_COLS], BF16, name="zeros")
         nc.gpsimd.memset(zeros[:], 0.0)
@@ -52,15 +52,15 @@ def tile_scatter_matmul_kernel(tc, base, x, w, offs, out):
         window = psum.tile([P, TOKENS], F32, name="window")
         nc.tensor.matmul(window[:], ident[:], base_sb[:], start=True, stop=False)
 
-        for kb in range(K_BLOCKS):
-            h, b = divmod(kb, HALF_BLOCKS)
-            for e in range(EXPERTS):
+        for e in range(EXPERTS):
+            for kb in range(K_BLOCKS):
+                h, b = divmod(kb, HALF_BLOCKS)
                 nc.tensor.matmul(
                     window[:].indirect(offsets[:, e * PIECE_COLS : (e + 1) * PIECE_COLS]),
-                    w_sb[h][:, e, b, :],
+                    w_sb[e][:, kb, :],
                     x_sb[h][:, b, e * PIECE : (e + 1) * PIECE],
                     start=False,
-                    stop=(kb == K_BLOCKS - 1 and e == EXPERTS - 1),
+                    stop=(e == EXPERTS - 1 and kb == K_BLOCKS - 1),
                 )
 
         z_sb = held.tile([P, TOKENS], F32, name="z_sb")

@@ -25,20 +25,18 @@ def tile_scatter_matmul_kernel(tc, base, x, w, offs, out):
         tc.psum_pool(name="psum", bufs=1) as psum,
     ):
         base_sb = held.tile([P, TOKENS], BF16, name="base_sb")
-        nc.sync.dma_start(base_sb[:], base)
-
         offsets = held.tile([P, TOKENS // 16], U16, name="offsets")
-        nc.sync.dma_start(offsets[:], offs)
 
         x_view = x.rearrange("(p kb) n -> p kb n", kb=K_BLOCKS)
         w_view = w.rearrange("e (p kb) m -> p e kb m", kb=K_BLOCKS)
-        x_sb, w_sb = [], []
-        for i in range(HALVES):
-            blocks = slice(i * HALF_BLOCKS, (i + 1) * HALF_BLOCKS)
-            x_sb.append(held.tile([P, HALF_BLOCKS, TOKENS], BF16, name="x_sb%d" % i))
-            nc.sync.dma_start(x_sb[i][:], x_view[:, blocks, :])
-            w_sb.append(held.tile([P, K_BLOCKS, P], BF16, name="w_sb%d" % i))
-            nc.sync.dma_start(w_sb[i][:], w_view[:, i, :, :])
+        x_sb = [held.tile([P, HALF_BLOCKS, TOKENS], BF16, name="x_sb%d" % h) for h in range(HALVES)]
+        w_sb = [held.tile([P, K_BLOCKS, P], BF16, name="w_sb%d" % e) for e in range(EXPERTS)]
+        nc.sync.dma_start(x_sb[0][:], x_view[:, 0:HALF_BLOCKS, :])
+        nc.sync.dma_start(base_sb[:], base)
+        nc.sync.dma_start(w_sb[0][:], w_view[:, 0, :, :])
+        nc.sync.dma_start(offsets[:], offs)
+        nc.sync.dma_start(x_sb[1][:], x_view[:, HALF_BLOCKS:K_BLOCKS, :])
+        nc.sync.dma_start(w_sb[1][:], w_view[:, 1, :, :])
 
         zeros = held.tile([P, WARM_COLS], BF16, name="zeros")
         nc.gpsimd.memset(zeros[:], 0.0)

@@ -39,7 +39,7 @@ def tile_scatter_matmul_kernel(tc, base, x, w, offs, out):
         nc.sync.dma_start(w_sb[1][:], w_view[:, 1, :, :])
 
         zeros = held.tile([P, WARM_COLS], BF16, name="zeros")
-        nc.gpsimd.memset(zeros[:], 0.0)
+        nc.vector.memset(zeros[:], 0.0)
         warm = psum.tile([P, WARM_COLS], F32, name="warm")
         for i in range(WARM_MATMULS):
             nc.tensor.matmul(warm[:], zeros[:, 0:P], zeros[:], start=True, stop=True)

@@ -35,8 +35,9 @@ def tile_scatter_matmul_kernel(tc, base, x, w, offs, out):
         nc.sync.dma_start(base_sb[:], base)
         nc.sync.dma_start(w_sb[0][:], w_view[:, 0, :, :])
         nc.sync.dma_start(offsets[:], offs)
+        nc.sync.dma_start(w_sb[1][:, 0:HALF_BLOCKS, :], w_view[:, 1, 0:HALF_BLOCKS, :])
         nc.sync.dma_start(x_sb[1][:], x_view[:, HALF_BLOCKS:K_BLOCKS, :])
-        nc.sync.dma_start(w_sb[1][:], w_view[:, 1, :, :])
+        nc.sync.dma_start(w_sb[1][:, HALF_BLOCKS:K_BLOCKS, :], w_view[:, 1, HALF_BLOCKS:K_BLOCKS, :])
 
         zeros = held.tile([P, WARM_COLS], BF16, name="zeros")
         nc.vector.memset(zeros[:], 0.0)
@@ -50,16 +51,16 @@ def tile_scatter_matmul_kernel(tc, base, x, w, offs, out):
         window = psum.tile([P, TOKENS], F32, name="window")
         nc.tensor.matmul(window[:], ident[:], base_sb[:], start=True, stop=False)
 
-        for e in range(EXPERTS):
-            for kb in range(K_BLOCKS):
-                h, b = divmod(kb, HALF_BLOCKS)
-                nc.tensor.matmul(
-                    window[:].indirect(offsets[:, e * PIECE_COLS : (e + 1) * PIECE_COLS]),
-                    w_sb[e][:, kb, :],
-                    x_sb[h][:, b, e * PIECE : (e + 1) * PIECE],
-                    start=False,
-                    stop=(e == EXPERTS - 1 and kb == K_BLOCKS - 1),
-                )
+        for h in range(HALVES):
+            for e in range(EXPERTS):
+                for b in range(HALF_BLOCKS):
+                    nc.tensor.matmul(
+                        window[:].indirect(offsets[:, e * PIECE_COLS : (e + 1) * PIECE_COLS]),
+                        w_sb[e][:, h * HALF_BLOCKS + b, :],
+                        x_sb[h][:, b, e * PIECE : (e + 1) * PIECE],
+                        start=False,
+                        stop=(h == HALVES - 1 and e == EXPERTS - 1 and b == HALF_BLOCKS - 1),
+                    )
 
         z_sb = held.tile([P, TOKENS], F32, name="z_sb")
         nc.vector.tensor_copy(z_sb[:], window[:])

@@ -33,11 +33,11 @@ def tile_scatter_matmul_kernel(tc, base, x, w, offs, out):
         w_sb = [held.tile([P, K_BLOCKS, P], BF16, name="w_sb%d" % e) for e in range(EXPERTS)]
         nc.sync.dma_start(x_sb[0][:], x_view[:, 0:HALF_BLOCKS, :])
         nc.sync.dma_start(base_sb[:], base)
-        nc.sync.dma_start(w_sb[0][:], w_view[:, 0, :, :])
+        nc.sync.dma_start(w_sb[0][:, 0:HALF_BLOCKS, :], w_view[:, 0, 0:HALF_BLOCKS, :])
         nc.sync.dma_start(offsets[:], offs)
-        nc.sync.dma_start(w_sb[1][:, 0:HALF_BLOCKS, :], w_view[:, 1, 0:HALF_BLOCKS, :])
+        nc.sync.dma_start(w_sb[1][:], w_view[:, 1, :, :])
         nc.sync.dma_start(x_sb[1][:], x_view[:, HALF_BLOCKS:K_BLOCKS, :])
-        nc.sync.dma_start(w_sb[1][:, HALF_BLOCKS:K_BLOCKS, :], w_view[:, 1, HALF_BLOCKS:K_BLOCKS, :])
+        nc.sync.dma_start(w_sb[0][:, HALF_BLOCKS:K_BLOCKS, :], w_view[:, 0, HALF_BLOCKS:K_BLOCKS, :])
 
         zeros = held.tile([P, WARM_COLS], BF16, name="zeros")
         nc.vector.memset(zeros[:], 0.0)
@@ -51,16 +51,16 @@ def tile_scatter_matmul_kernel(tc, base, x, w, offs, out):
         window = psum.tile([P, TOKENS], F32, name="window")
         nc.tensor.matmul(window[:], ident[:], base_sb[:], start=True, stop=False)
 
-        for h in range(HALVES):
-            for e in range(EXPERTS):
-                for b in range(HALF_BLOCKS):
-                    nc.tensor.matmul(
-                        window[:].indirect(offsets[:, e * PIECE_COLS : (e + 1) * PIECE_COLS]),
-                        w_sb[e][:, h * HALF_BLOCKS + b, :],
-                        x_sb[h][:, b, e * PIECE : (e + 1) * PIECE],
-                        start=False,
-                        stop=(h == HALVES - 1 and e == EXPERTS - 1 and b == HALF_BLOCKS - 1),
-                    )
+        pairs = ((0, 0), (0, 1), (1, 1), (1, 0))
+        for h, e in pairs:
+            for b in range(HALF_BLOCKS):
+                nc.tensor.matmul(
+                    window[:].indirect(offsets[:, e * PIECE_COLS : (e + 1) * PIECE_COLS]),
+                    w_sb[e][:, h * HALF_BLOCKS + b, :],
+                    x_sb[h][:, b, e * PIECE : (e + 1) * PIECE],
+                    start=False,
+                    stop=((h, e) == pairs[-1] and b == HALF_BLOCKS - 1),
+                )
 
         z_sb = held.tile([P, TOKENS], F32, name="z_sb")
         nc.vector.tensor_copy(z_sb[:], window[:])

@@ -13,7 +13,9 @@ PIECE = TOKENS // EXPERTS
 PIECE_COLS = PIECE // 16
 
 WARM_COLS = 128
-WARM_MATMULS = 10
+COL_TILE = 32
+COL_TILES = P // COL_TILE
+WARM_ROUNDS = 8
 
 FLOPS = 2 * K_BLOCKS * P * P * TOKENS
 
@@ -42,8 +44,11 @@ def tile_scatter_matmul_kernel(tc, base, x, w, offs, out):
         zeros = held.tile([P, WARM_COLS], BF16, name="zeros")
         nc.vector.memset(zeros[:], 0.0)
         warm = psum.tile([P, WARM_COLS], F32, name="warm")
-        for i in range(WARM_MATMULS):
-            nc.tensor.matmul(warm[:], zeros[:, 0:P], zeros[:], start=True, stop=True)
+        for i in range(WARM_ROUNDS):
+            for j in range(COL_TILES):
+                nc.tensor.matmul(
+                    warm[j * COL_TILE : (j + 1) * COL_TILE, :], zeros[:, 0:COL_TILE], zeros[:], start=True, stop=True
+                )
 
         ident = held.tile([P, P], BF16, name="ident")
         make_identity(nc, ident[:])

@@ -12,6 +12,8 @@ HALF_BLOCKS = K_BLOCKS // HALVES
 PIECE = TOKENS // EXPERTS
 PIECE_COLS = PIECE // 16
 
+DMA_ALIGN = 1024
+
 WARM_COLS = 128
 COL_TILE = 32
 COL_TILES = P // COL_TILE
@@ -26,13 +28,15 @@ def tile_scatter_matmul_kernel(tc, base, x, w, offs, out):
         tc.tile_pool(name="held", bufs=1) as held,
         tc.psum_pool(name="psum", bufs=1) as psum,
     ):
-        base_sb = held.tile([P, TOKENS], BF16, name="base_sb")
+        base_sb = held.tile([P, TOKENS], BF16, name="base_sb", align_bytes=DMA_ALIGN)
         offsets = held.tile([P, TOKENS // 16], U16, name="offsets")
 
         x_view = x.rearrange("(p kb) n -> p kb n", kb=K_BLOCKS)
         w_view = w.rearrange("e (p kb) m -> p e kb m", kb=K_BLOCKS)
-        x_sb = [held.tile([P, HALF_BLOCKS, TOKENS], BF16, name="x_sb%d" % h) for h in range(HALVES)]
-        w_sb = [held.tile([P, K_BLOCKS, P], BF16, name="w_sb%d" % e) for e in range(EXPERTS)]
+        x_sb = [
+            held.tile([P, HALF_BLOCKS, TOKENS], BF16, name="x_sb%d" % h, align_bytes=DMA_ALIGN) for h in range(HALVES)
+        ]
+        w_sb = [held.tile([P, K_BLOCKS, P], BF16, name="w_sb%d" % e, align_bytes=DMA_ALIGN) for e in range(EXPERTS)]
         nc.sync.dma_start(x_sb[0][:], x_view[:, 0:HALF_BLOCKS, :])
         nc.sync.dma_start(base_sb[:], base)
         nc.sync.dma_start(w_sb[0][:, 0:HALF_BLOCKS, :], w_view[:, 0, 0:HALF_BLOCKS, :])
@@ -41,13 +45,17 @@ def tile_scatter_matmul_kernel(tc, base, x, w, offs, out):
         nc.sync.dma_start(x_sb[1][:], x_view[:, HALF_BLOCKS:K_BLOCKS, :])
         nc.sync.dma_start(w_sb[0][:, HALF_BLOCKS:K_BLOCKS, :], w_view[:, 0, HALF_BLOCKS:K_BLOCKS, :])
 
-        zeros = held.tile([P, WARM_COLS], BF16, name="zeros")
+        zeros = held.tile([P, WARM_COLS + 1], BF16, name="zeros")
         nc.vector.memset(zeros[:], 0.0)
         warm = psum.tile([P, WARM_COLS], F32, name="warm")
         for i in range(WARM_ROUNDS):
             for j in range(COL_TILES):
                 nc.tensor.matmul(
-                    warm[j * COL_TILE : (j + 1) * COL_TILE, :], zeros[:, 0:COL_TILE], zeros[:], start=True, stop=True
+                    warm[j * COL_TILE : (j + 1) * COL_TILE, :],
+                    zeros[:, 0:COL_TILE],
+                    zeros[:, 0:WARM_COLS],
+                    start=True,
+                    stop=True,
                 )
 
         ident = held.tile([P, P], BF16, name="ident")
@@ -67,6 +75,6 @@ def tile_scatter_matmul_kernel(tc, base, x, w, offs, out):
                     stop=((h, e) == pairs[-1] and b == HALF_BLOCKS - 1),
                 )
 
-        z_sb = held.tile([P, TOKENS], F32, name="z_sb")
+        z_sb = held.tile([P, TOKENS], F32, name="z_sb", align_bytes=DMA_ALIGN)
         nc.vector.tensor_copy(z_sb[:], window[:])
         nc.sync.dma_start(out, z_sb[:])

import concourse.mybir as mybir
from concourse.masks import make_identity

BF16, F32, U16 = mybir.dt.bfloat16, mybir.dt.float32, mybir.dt.uint16

P = 128
TOKENS = 256
K_BLOCKS = 4
EXPERTS = 2
HALVES = 2
HALF_BLOCKS = K_BLOCKS // HALVES
PIECE = TOKENS // EXPERTS
PIECE_COLS = PIECE // 16

DMA_ALIGN = 1024

WARM_COLS = 128
COL_TILE = 32
COL_TILES = P // COL_TILE
WARM_ROUNDS = 8

FLOPS = 2 * K_BLOCKS * P * P * TOKENS


def tile_scatter_matmul_kernel(tc, base, x, w, offs, out):
    nc = tc.nc
    with (
        tc.tile_pool(name="held", bufs=1) as held,
        tc.psum_pool(name="psum", bufs=1) as psum,
    ):
        base_sb = held.tile([P, TOKENS], BF16, name="base_sb", align_bytes=DMA_ALIGN)
        offsets = held.tile([P, TOKENS // 16], U16, name="offsets")

        x_view = x.rearrange("(p kb) n -> p kb n", kb=K_BLOCKS)
        w_view = w.rearrange("e (p kb) m -> p e kb m", kb=K_BLOCKS)
        x_sb = [
            held.tile([P, HALF_BLOCKS, TOKENS], BF16, name="x_sb%d" % h, align_bytes=DMA_ALIGN) for h in range(HALVES)
        ]
        w_sb = [held.tile([P, K_BLOCKS, P], BF16, name="w_sb%d" % e, align_bytes=DMA_ALIGN) for e in range(EXPERTS)]
        nc.sync.dma_start(x_sb[0][:], x_view[:, 0:HALF_BLOCKS, :])
        nc.sync.dma_start(base_sb[:], base)
        nc.sync.dma_start(w_sb[0][:, 0:HALF_BLOCKS, :], w_view[:, 0, 0:HALF_BLOCKS, :])
        nc.sync.dma_start(offsets[:], offs)
        nc.sync.dma_start(w_sb[1][:], w_view[:, 1, :, :])
        nc.sync.dma_start(x_sb[1][:], x_view[:, HALF_BLOCKS:K_BLOCKS, :])
        nc.sync.dma_start(w_sb[0][:, HALF_BLOCKS:K_BLOCKS, :], w_view[:, 0, HALF_BLOCKS:K_BLOCKS, :])

        zeros = held.tile([P, WARM_COLS + 1], BF16, name="zeros")
        nc.vector.memset(zeros[:], 0.0)
        warm = psum.tile([P, WARM_COLS], F32, name="warm")
        for i in range(WARM_ROUNDS):
            for j in range(COL_TILES):
                nc.tensor.matmul(
                    warm[j * COL_TILE : (j + 1) * COL_TILE, :],
                    zeros[:, 0:COL_TILE],
                    zeros[:, 0:WARM_COLS],
                    start=True,
                    stop=True,
                )

        ident = held.tile([P, P], BF16, name="ident")
        make_identity(nc, ident[:])

        window = psum.tile([P, TOKENS], F32, name="window")
        nc.tensor.matmul(window[:], ident[:], base_sb[:], start=True, stop=False)

        pairs = ((0, 0), (0, 1), (1, 1), (1, 0))
        for h, e in pairs:
            for b in range(HALF_BLOCKS):
                nc.tensor.matmul(
                    window[:].indirect(offsets[:, e * PIECE_COLS : (e + 1) * PIECE_COLS]),
                    w_sb[e][:, h * HALF_BLOCKS + b, :],
                    x_sb[h][:, b, e * PIECE : (e + 1) * PIECE],
                    start=False,
                    stop=((h, e) == pairs[-1] and b == HALF_BLOCKS - 1),
                )

        z_sb = held.tile([P, TOKENS], F32, name="z_sb", align_bytes=DMA_ALIGN)
        nc.vector.tensor_copy(z_sb[:], window[:])
        nc.sync.dma_start(out, z_sb[:])
